import numpy as np, ml_dtypes
CORES = [17,57,65,89,97,121]
N = 6
T, SQ = 2048, 1024
def entries(a): return a.T.reshape(-1)
def pack(v, P): return np.ascontiguousarray(np.asarray(v, np.int32).reshape(-1, P).T)
def lists(rng, how):
    h = N // 2; d = rng.integers(0, SQ, h); n = np.full(N, SQ); p = rng.permutation(N); n[p[0:2 * h:2]] += d; n[p[1:2 * h:2]] -= d
    if how == "back": g = int(rng.integers(2, h + 1)); n[:] = 0; n[N - g:] = T
    if how == "ends": d = rng.integers(SQ // 4, SQ - 1, h); n[:] = SQ; n[:h] += d; n[N - h:] -= d
    if how == "front": n[:] = 0; n[:h] = T; n[h] = (N - 2 * h) * SQ
    if how == "late": n[:] = 0; n[int(rng.integers(N - 1))] = int(rng.integers(1, SQ)); n[N - 1] = T
    if how == "tail": g = min(3, N // 3); n = rng.integers(SQ // 8, SQ // 4, N); n[N - g:] = T - n[N - g:]
    F = np.zeros((N, T), np.int64)
    for r in range(N):
        o = rng.permutation(T)
        if how == "ends": o = np.concatenate([[0, T - 1], 1 + rng.permutation(T - 2)])
        F[r, o[:n[r]]] = 1
    return {"fl": np.stack([pack(f, 16) for f in F])}
def setup_inputs(rng):
    return dict({"x": rng.standard_normal((N, 128, T), dtype=np.float32).astype(ml_dtypes.bfloat16), "st": rng.standard_normal((N, 128, SQ), dtype=np.float32).astype(ml_dtypes.bfloat16)}, **lists(rng, "uniform"))
def setup_inputs_back(rng):
    d = setup_inputs(rng); d.update(lists(rng, "back"))
    for k in ("x", "st"): d[k] = (d[k].astype(np.float32) * 1048576.0).astype(d[k].dtype)
    return d
def setup_inputs_ends(rng):
    d = setup_inputs(rng); d.update(lists(rng, "ends"))
    for k in ("x", "st"): d[k] = (d[k].astype(np.float32) * (1 / 1024.0)).astype(d[k].dtype)
    return d
def setup_inputs_front(rng):
    d = setup_inputs(rng); d.update(lists(rng, "front"))
    return d
def setup_inputs_late(rng):
    d = setup_inputs(rng); d.update(lists(rng, "late"))
    return d
def setup_inputs_tail(rng):
    d = setup_inputs(rng); d.update(lists(rng, "tail"))
    return d
def check_inputs(x):
    bad = []
    if x["fl"].min() < 0 or x["fl"].max() >= 2: bad.append("fl out of range")
    if int(x["fl"].sum()) > N * SQ: bad.append("more flags than the stream has columns")
    return bad
def reference(x, st, fl):
    S = np.concatenate(list(st), axis=1); X = np.concatenate(list(x), axis=1)
    F = np.concatenate([entries(f) for f in fl]) > 0; c = np.cumsum(F) - F
    Y = np.where(F[None, :], S[:, np.minimum(c, N * SQ - 1)], X)
    return {"y": np.stack([Y[:, T * r:T * r + T] for r in range(N)])}

from concourse.bass import DstId, RemoteDMATransfer
from concourse.mybir import AluOpType, AxisListType, ActivationFunctionType

N, TC, SQ = 6, 2048, 1024
NCORES = 128
HELPERS = 3
SW = 352
SLICES = [(0, 0, 352), (336, 352, 688), (672, 688, SQ)]
BIG = 8192.0
CHUNKS = [(0, 640), (640, 1024)]

SCRATCH = {
    "W": ("sbuf", [128, TC + N * SQ], "bfloat16"),
    "Y": ("sbuf", [128, TC], "bfloat16"),
    "FD": ("dram", [128, 16], "int32"),
    "FR": ("sbuf", [128, 16 * N], "int32"),
    "FRB": ("sbuf", [128, 16 * N], "bfloat16"),
    "FLI": ("sbuf", [16, 128], "int32"),
    "FB": ("sbuf", [16, 128], "bfloat16"),
    "U1": ("sbuf", [16, 128], "float32"),
    "U2": ("sbuf", [16, 128], "float32"),
    "J": ("sbuf", [16, 128], "float32"),
    "ONES": ("sbuf", [128, 128], "bfloat16"),
    "NEG": ("sbuf", [16, 128], "bfloat16"),
    "ONEF": ("sbuf", [16, 128], "float32"),
    "LOW": ("sbuf", [16, 128], "bfloat16"),
    "EYE": ("sbuf", [16, 128], "float32"),
    "ZERO": ("sbuf", [128, 128], "float32"),
    "S": ("sbuf", [128, 128], "float32"),
    "E": ("sbuf", [128, 128], "float32"),
    "EB": ("sbuf", [128, 128], "float32"),
    "OF": ("sbuf", [128, 128], "float32"),
    "BASE": ("sbuf", [128, 1], "float32"),
    "OFF": ("sbuf", [128, 128], "uint16"),
    "P1": ("psum", [128, 512], "float32"),
    "P2": ("psum", [128, 512], "float32"),
    "P3": ("psum", [128, 512], "float32"),
    "P4": ("psum", [128, 512], "float32"),
}
SEMAPHORES = ["fl_ld", "st_ld", "x_ld", "f16_ld", "c_ones", "c_neg", "c_onef", "c_zero", "c_low", "c_eye", "c_j",
              "s_fb", "s_u1", "s_u2", "s_p1", "s_p2", "s_p3", "s_s", "s_e", "s_frb", "s_p4", "s_b", "s_eb", "s_of", "s_off",
              "gv0", "gv1", "gs0", "gs1", "yv0", "yv1", "ys0", "ys1",
              "flag_h", "data_h", "flag_a", "data_a", "sent"]


def engines(topo, src, dst):
    m = topo.mask(src, dst)
    return [e for e in range(m.bit_length()) if (m >> e) & 1]


def bits(es):
    return sum(1 << e for e in es)


def needs(d):
    return range(min(N, 2 * (d + 1)))


def plan(T, topo):
    P = []
    for p in range(N):
        c = T.cores[p]
        want = [(p + k) % N for k in range(1, N)]
        want = [d for d in want if p in needs(d)]
        direct = [d for d in want if topo.may_write(c, T.cores[d])]
        far = [d for d in want if d not in direct]
        able = [h for h in range(NCORES) if h != c and topo.chip(h) == topo.chip(c)
                and all(topo.may_write(h, T.cores[d]) for d in range(N) if d != p)]
        near_die = [h for h in able if topo.die(h) == topo.die(c)]
        far_die = [h for h in able if topo.die(h) != topo.die(c)]
        help3 = far_die[:2] + near_die[:1]
        later = [d for d in range(N) if d > p]
        flags = [later[k::HELPERS] for k in range(HELPERS)]
        P.append({"core": c, "direct": direct, "far": far, "help": help3, "flags": flags})
    return P


def dsts(topo, cores):
    return [DstId(rid=topo.addr(c)[0], pnc=topo.addr(c)[1]) for c in cores]


def part(T, p, a=0, b=SQ):
    return T.W[:, TC + p * SQ + a:TC + p * SQ + b]


def forwarder(g, core, T, topo, P, p, k):
    sem, me = T.sem, P[p]
    hop = len(onchip(topo, me["core"], me["help"])[k])
    sent = 0
    if me["flags"][k]:
        to = [T.cores[d] for d in me["flags"][k]]
        es = min((engines(topo, core, t) for t in to), key=len)
        g.wait_ge(sem.flag_h, hop)
        g.remote_dma_fused([RemoteDMATransfer(dst_ids=dsts(topo, to), dma_engine_mask=bits(es), remote_sem=sem.flag_a,
                                              srcs=[T.FD[:]], dsts=[T.FR[:, 16 * p:16 * p + 16] for t in to])],
                           local_sem=sem.sent)
        sent += len(es)
    if me["far"]:
        to = [T.cores[d] for d in me["far"]]
        es = min((engines(topo, core, t) for t in to), key=len)
        a, b = SLICES[k][1:]
        g.wait_ge(sem.data_h, hop)
        g.remote_dma_fused([RemoteDMATransfer(dst_ids=dsts(topo, to), dma_engine_mask=bits(es), remote_sem=sem.data_a,
                                              srcs=[part(T, p, a, b)], dsts=[part(T, p, a, b) for t in to])],
                           local_sem=sem.sent)
        sent += len(es)
    g.wait_ge(sem.sent, sent)


def onchip(topo, core, helpers):
    es = engines(topo, core, helpers[0])[::-1]
    return [es[4 * k:4 * k + 4] for k in range(len(helpers))]


def rank_program(g, core, T, topo):
    P = plan(T, topo)
    rank = T.rank_of(core)
    if rank is None:
        for p in range(N):
            if core in P[p]["help"]:
                forwarder(g, core, T, topo, P, p, P[p]["help"].index(core))
        return
    sem, me = T.sem, P[rank]
    v, t, s, y = g.vector, g.tensor, g.scalar, g.sync
    A = AluOpType

    y.dma_start(T.FD[:], T.fl[:]).then_inc(sem.fl_ld, 16)
    y.dma_start(part(T, rank), T.st[:]).then_inc(sem.st_ld, 16)
    s.dma_start(T.FLI[:], T.fl[:]).then_inc(sem.f16_ld, 16)
    s.wait_ge(sem.fl_ld, 16)
    s.dma_start(T.W[:, 0:TC], T.x[:]).then_inc(sem.x_ld, 16)

    v.memset(T.NEG[:], -1.0).then_inc(sem.c_neg, 1)
    v.memset(T.ONEF[:], 1.0).then_inc(sem.c_onef, 1)
    v.memset(T.ONES[:], 1.0).then_inc(sem.c_ones, 1)
    v.memset(T.ZERO[:], 0.0).then_inc(sem.c_zero, 1)
    g.wait_ge(sem.c_neg, 1)
    g.affine_select(T.LOW[:], T.NEG[:], [[0, 8], [-1, 16]], A.is_ge, 0.0, 0, 1).then_inc(sem.c_low, 1)
    g.wait_ge(sem.c_onef, 1)
    g.affine_select(T.EYE[:], T.ONEF[:], [[0, 8], [-1, 16]], A.is_equal, 0.0, 0, 1).then_inc(sem.c_eye, 1)
    g.iota(T.J[:], [[16, 128]], 0, 1, allow_small_or_imprecise_dtypes=True).then_inc(sem.c_j, 1)

    sent = 0
    groups = onchip(topo, core, me["help"])
    busy = [k for k in range(HELPERS) if me["flags"][k]]
    if busy:
        g.wait_ge(sem.fl_ld, 16)
        g.remote_dma_fused([RemoteDMATransfer(dst_ids=dsts(topo, [me["help"][k]]), dma_engine_mask=bits(groups[k]),
                                              remote_sem=sem.flag_h, srcs=[T.FD[:]], dsts=[T.FD[:]]) for k in busy],
                           local_sem=sem.sent)
        sent += sum(len(groups[k]) for k in busy)
    g.wait_ge(sem.st_ld, 16)
    if me["far"]:
        g.remote_dma_fused([RemoteDMATransfer(dst_ids=dsts(topo, [me["help"][k]]), dma_engine_mask=bits(groups[k]),
                                              remote_sem=sem.data_h, srcs=[part(T, rank, SLICES[k][0], SLICES[k][0] + SW)],
                                              dsts=[part(T, rank, SLICES[k][0], SLICES[k][0] + SW)]) for k in range(HELPERS)],
                           local_sem=sem.sent)
        sent += sum(len(x) for x in groups)
    if me["direct"]:
        to = [T.cores[d] for d in me["direct"]]
        es = min((engines(topo, core, c) for c in to), key=len)
        g.remote_dma_fused([RemoteDMATransfer(dst_ids=dsts(topo, to), dma_engine_mask=bits(es), remote_sem=sem.data_a,
                                              srcs=[part(T, rank)], dsts=[part(T, rank) for c in to])], local_sem=sem.sent)
        sent += len(es)

    v.wait_ge(sem.f16_ld, 16)
    v.tensor_copy(T.FB[:], T.FLI[:]).then_inc(sem.s_fb, 1)
    v.tensor_scalar(T.U1[:], T.FLI[:], BIG, None, A.mult).then_inc(sem.s_u1, 1)
    v.wait_ge(sem.s_u1, 1)
    v.wait_ge(sem.c_j, 1)
    v.tensor_tensor(T.U2[:], T.U1[:], T.J[:], A.add).then_inc(sem.s_u2, 1)
    t.wait_ge(sem.c_ones, 1)
    t.wait_ge(sem.s_fb, 1)
    t.matmul(T.P1[:, 0:128], T.ONES[0:16, :], T.FB[:], True, True).then_inc(sem.s_p1, 1)
    t.wait_ge(sem.c_low, 1)
    t.matmul(T.P2[:, 0:128], T.LOW[:], T.FB[:], True, True).then_inc(sem.s_p2, 1)
    t.wait_ge(sem.c_eye, 1)
    t.wait_ge(sem.s_u2, 1)
    t.matmul(T.P3[:, 0:128], T.EYE[:], T.U2[:], True, True).then_inc(sem.s_p3, 1)
    v.wait_ge(sem.c_zero, 1)
    v.wait_ge(sem.s_p1, 1)
    v.tensor_tensor_scan(T.S[:], T.P1[:, 0:128], T.ZERO[:], float(TC), A.add, A.add).then_inc(sem.s_s, 1)
    v.wait_ge(sem.s_s, 1)
    v.wait_ge(sem.s_p2, 1)
    v.tensor_tensor(T.E[:], T.S[:], T.P2[:, 0:128], A.add).then_inc(sem.s_e, 1)
    v.wait_ge(sem.s_e, 1)
    e = T.E
    if rank > 0:
        n = 16 * rank
        arrive = 0
        for p in range(rank):
            for k in range(HELPERS):
                if rank in P[p]["flags"][k]:
                    to = [T.cores[d] for d in P[p]["flags"][k]]
                    arrive += min(len(engines(topo, P[p]["help"][k], c)) for c in to)
        v.wait_ge(sem.flag_a, arrive)
        v.tensor_copy(T.FRB[:, 0:n], T.FR[:, 0:n]).then_inc(sem.s_frb, 1)
        t.wait_ge(sem.s_frb, 1)
        t.matmul(T.P4[:, 0:n], T.ONES[:], T.FRB[:, 0:n], True, True).then_inc(sem.s_p4, 1)
        v.wait_ge(sem.s_p4, 1)
        v.tensor_reduce(T.BASE[:], T.P4[:, 0:n], AxisListType.X, A.add).then_inc(sem.s_b, 1)
        v.wait_ge(sem.s_b, 1)
        v.tensor_scalar(T.EB[:], T.E[:], T.BASE[:], None, A.add).then_inc(sem.s_eb, 1)
        v.wait_ge(sem.s_eb, 1)
        e = T.EB
    v.wait_ge(sem.s_p3, 1)
    v.tensor_tensor(T.OF[:], e[:], T.P3[:, 0:128], A.min).then_inc(sem.s_of, 1)
    v.wait_ge(sem.s_of, 1)
    v.tensor_copy(T.OFF[:], T.OF[:]).then_inc(sem.s_off, 1)

    arrive = 0
    for p in needs(rank):
        if p == rank:
            continue
        if rank in P[p]["direct"]:
            arrive += min(len(engines(topo, P[p]["core"], T.cores[d])) for d in P[p]["direct"])
        else:
            arrive += sum(min(len(engines(topo, h, T.cores[d])) for d in P[p]["far"]) for h in P[p]["help"])
    end = TC + SQ * len(needs(rank))
    half = TC // 2
    for q in (v, s):
        q.wait_ge(sem.s_off, 1)
        q.wait_ge(sem.x_ld, 16)
        q.wait_ge(sem.st_ld, 16)
        q.wait_ge(sem.data_a, arrive)
    for i, (a, b) in enumerate(CHUNKS):
        v.tensor_copy(T.Y[:, a:b], T.W[:, 0:end].indirect(T.OFF[:, a // 16:b // 16])).then_inc(sem["gv%d" % i], 1)
        a, b = a + half, b + half
        s.activation(T.Y[:, a:b], T.W[:, 0:end].indirect(T.OFF[:, a // 16:b // 16]),
                     ActivationFunctionType.Copy).then_inc(sem["gs%d" % i], 1)
    last = len(CHUNKS) - 1
    for i, (a, b) in enumerate(CHUNKS):
        y.wait_ge(sem["gv%d" % i], 1)
        y.dma_start(T.y[:, a:b], T.Y[:, a:b]).then_inc(sem["yv%d" % i], 16)
        q = s if i == last else y
        a, b = a + half, b + half
        q.wait_ge(sem["gs%d" % i], 1)
        q.dma_start(T.y[:, a:b], T.Y[:, a:b]).then_inc(sem["ys%d" % i], 16)
    for i in range(len(CHUNKS)):
        y.wait_ge(sem["yv%d" % i], 16)
        y.wait_ge(sem["ys%d" % i], 16)
    g.wait_ge(sem.sent, sent)
